import numpy as np
import ml_dtypes


def mxq(x, axis, fmt="e4m3"):
    dtype, down = {"e4m3": (ml_dtypes.float8_e4m3fn, 7), "e5m2": (ml_dtypes.float8_e5m2, 14)}[fmt]
    v = np.moveaxis(np.asarray(x, np.float32).astype(ml_dtypes.bfloat16).astype(np.float64), axis, -1)
    blocks = v.reshape(v.shape[:-1] + (-1, 32))
    amax = np.abs(blocks).max(-1, keepdims=True)
    byte = np.maximum(np.where(amax > 0, np.frexp(amax)[1] - 1 + 127, 0) - down, 1)
    scale = np.exp2(byte - 127.0)
    codes = (blocks / scale).astype(np.float32).astype(dtype).astype(np.float64)
    return np.moveaxis((codes * scale).reshape(v.shape), -1, axis)


WIDE = False


def mx_kscale(k):
    if not WIDE:
        return np.ones(k)
    levels = np.array([10, -10, 5, -5, 0])
    if k % 512:
        return np.exp2(np.random.permutation(np.resize(levels, k // 32))).repeat(32)
    a = np.empty((k // 512, 16))
    for p in range(k // 512):
        a[p, :8] = np.random.permutation(np.resize(levels, 8))
        for g in range(8):
            far = levels[np.abs(levels - a[p, g]) >= 10]
            a[p, g + 8] = far[np.random.randint(len(far))]
    return np.exp2(a.ravel()).repeat(32)


BF16 = ml_dtypes.bfloat16


def bf(x):
    return np.asarray(x, np.float32).astype(BF16)


def f64(x):
    return np.asarray(x).astype(np.float64)


M, T, D, F = 16, 512, 512, 256

SHRINK = 0.8
STEP = 0.3


def shrink_scale(d, t):
    idx = np.arange(d)
    on_diag = idx[:, None] == idx[None, :]
    return np.where(on_diag, 1.0 / t, SHRINK / t)


def draw0():
    a, b = mx_kscale(T), mx_kscale(D)
    return {"x": bf(np.random.standard_normal((M, T, D))),
            "u": bf((1.0 + 0.1 * np.random.standard_normal((M, T))) * a),
            "v": bf((1.0 + 0.1 * np.random.standard_normal((M, T))) / a),
            "c": bf((1.0 + 0.1 * np.random.standard_normal((M, D))) * b),
            "tau": bf(np.random.standard_normal((M, D, F)) / b[:, None]),
            "w0": bf(np.random.standard_normal((D, F)))}


def core(x, u, v, c, tau, w0):
    x, u, v, c, tau, w0 = f64(x), f64(u), f64(v), f64(c), f64(tau), f64(w0)
    t = x.shape[1]
    d = x.shape[2]
    xu = mxq(u[:, :, None] * x, 1, "e4m3")
    xv = mxq(v[:, :, None] * x, 1, "e4m3")
    gram = xu.transpose(0, 2, 1) @ xv
    s = gram * shrink_scale(d, t)[None, :, :]
    p = s * c[:, None, :]
    r = mxq(p, 2, "e4m3") @ mxq(tau, 1, "e4m3")
    return w0 + STEP * np.sum(r, axis=0)


def e4m3fn_bytes(y):
    return np.clip(np.asarray(y, np.float64), -448.0, 448.0).astype(np.float32).astype(ml_dtypes.float8_e4m3fn).view(np.uint8)


def e4m3fn_values(b):
    return np.asarray(b, np.uint8).view(ml_dtypes.float8_e4m3fn).astype(np.float64)


def setup_inputs():
    d = draw0()
    x0 = np.asarray(d['tau']).astype(np.float64)
    s = (np.max(np.abs(x0), axis=(0, 2), keepdims=True) / 448.0).astype(np.float32)
    out = {}
    for k, v in d.items():
        if k == 'tau':
            out['tau_bytes'] = e4m3fn_bytes(x0 / s.astype(np.float64))
            out['tau_scale'] = s
        else:
            out[k] = v
    return out


def reference(x, u, v, c, tau_bytes, tau_scale, w0):
    return core(x, u, v, c, e4m3fn_values(tau_bytes) * tau_scale.astype(np.float64), w0)

@@ -1,0 +1,272 @@
+from contextlib import ExitStack
+
+import concourse.mybir as mybir
+from concourse.masks import make_identity
+
+MODELS, T, D, F = 16, 512, 512, 256
+FLOPS = 2 * MODELS * (T * D * D + D * D * F) + MODELS * (2 * T * D + 2 * D * D + D * F) + 2 * D * F
+
+P = 128
+K4 = 4
+SHRINK = 0.8
+STEP = 0.3
+
+F32 = mybir.dt.float32
+BF16 = mybir.dt.bfloat16
+U32 = mybir.dt.uint32
+U8 = mybir.dt.uint8
+FP8 = mybir.dt.float8_e4m3fn
+FP8X4 = mybir.dt.float8_e4m3fn_x4
+MULT = mybir.AluOpType.mult
+ADD = mybir.AluOpType.add
+COPY = mybir.ActivationFunctionType.Copy
+
+PE_COLS = 256
+V_PCOLS = 192
+
+
+def tile_regmeangramdescentmerge_t_kernel(tc, x, u, v, c, tau_bytes, tau_scale, w0, out):
+    nc = tc.nc
+    with ExitStack() as ctx:
+        const = ctx.enter_context(tc.tile_pool(name="const", bufs=1))
+        xin = ctx.enter_context(tc.tile_pool(name="xin", bufs=MODELS))
+        work = ctx.enter_context(tc.tile_pool(name="work", bufs=2))
+        psum = ctx.enter_context(tc.psum_pool(name="psum", bufs=2))
+        racc = ctx.enter_context(tc.psum_pool(name="racc", bufs=1))
+
+        gains = const.tile([P, D], BF16, name="gains")
+        nc.vector.memset(gains[:].bitcast(mybir.dt.int32), 0)
+        nc.scalar.dma_start(out=gains[0:16, :], in_=u)
+        nc.scalar.dma_start(out=gains[16:32, :], in_=v)
+        nc.scalar.dma_start(out=gains[32:48, :], in_=c)
+        tscale = const.tile([P, K4], F32, name="tscale")
+        nc.scalar.dma_start(out=tscale[:], in_=tau_scale.rearrange("o (p t) z -> p (o t z)", t=K4))
+
+        xt = []
+        tb = []
+
+        def load_x(i):
+            tile = xin.tile([P, K4, D], BF16, name="xt", tag="xt")
+            nc.sync.dma_start(out=tile[:], in_=x[i].rearrange("(p t) d -> p t d", t=K4))
+            xt.append(tile)
+
+        def load_tau(j):
+            tile = const.tile([P, 4, K4 * F], U8, name="tb%d" % j, tag="tb%d" % j)
+            nc.sync.dma_start(out=tile[:], in_=tau_bytes[4 * j:4 * j + 4].rearrange("i (p t) f -> p i (t f)", t=K4))
+            tb.append(tile)
+
+        load_x(0)
+        load_x(1)
+        load_tau(0)
+        for i in range(2, 6):
+            load_x(i)
+        load_tau(1)
+        for i in range(6, 10):
+            load_x(i)
+        load_tau(2)
+        for i in range(10, 14):
+            load_x(i)
+        load_tau(3)
+        for i in range(14, 16):
+            load_x(i)
+        w0t = const.tile([P, K4, F], BF16, name="w0t")
+        nc.sync.dma_start(out=w0t[:], in_=w0.rearrange("(q s) f -> q s f", s=K4))
+
+        ident = const.tile([P, P], BF16, name="ident")
+        make_identity(nc, ident[:])
+        dmask = const.tile([P, P], F32, name="dmask")
+        nc.vector.tensor_scalar(out=dmask[:], in0=ident[:], scalar1=1.0 / SHRINK - 1.0, scalar2=1.0, op0=MULT, op1=ADD)
+
+        warm = const.tile([P, 1], F32, name="warm")
+        nc.scalar.activation(out=warm[:], in_=ident[:, 0:1], func=COPY)
+
+        gp = psum.tile([P, K4, P], BF16, name="gp", tag="xp")
+        for t in range(K4):
+            nc.tensor.transpose(gp[:, t, :], gains[:, t:D:K4], ident[:])
+        uv = const.tile([P, 2 * MODELS, K4], BF16, name="uv")
+        nc.vector.tensor_copy(out=uv[:], in_=gp[:, :, 0:32].rearrange("p t r -> p r t"))
+        cs = const.tile([P, MODELS, K4], F32, name="cs")
+        nc.vector.tensor_scalar(out=cs[:], in0=gp[:, :, 32:48].rearrange("p t r -> p r t"), scalar1=SHRINK / T, scalar2=None, op0=MULT)
+
+        r = [racc.tile([P, F], F32, name="r%d" % s, tag="r%d" % s) for s in range(K4)]
+
+        st = {}
+
+        def ident_x(i):
+            xp = psum.tile([P, PE_COLS * K4], BF16, name="xp", tag="xp")
+            for h in range(PE_COLS // P):
+                nc.tensor.matmul(xp[:, 512 * h:512 * (h + 1)], lhsT=ident[:],
+                                 rhs=xt[i][:, :, P * h:P * (h + 1)].rearrange("p t d -> p d t"), start=True, stop=True)
+            st["xp", i] = xp
+
+        def scal_x(i):
+            n = D - PE_COLS
+            xs = work.tile([P, n * K4], BF16, name="xs", tag="xs")
+            nc.scalar.copy(out=xs[:].rearrange("p (c i t) -> p c t i", i=4, t=K4),
+                           in_=xt[i][:, :, PE_COLS:D].rearrange("p t (c i) -> p c t i", i=4))
+            st["xs", i] = xs
+
+        def gain_p(i, which):
+            g = work.tile([P, K4, P, K4], BF16, name="g" + which, tag="g" + which, align_bytes=64)
+            st["g" + which, i] = g
+            row = i + (0 if which == "u" else MODELS)
+            q = PE_COLS // K4
+            nc.vector.tensor_tensor(out=g[:, :, 0:q, :], in0=st["xp", i][:].rearrange("p (q s t) -> p s q t", s=K4, t=K4),
+                                    in1=uv[:, row:row + 1, :].unsqueeze(1).to_broadcast([P, K4, q, K4]), op=MULT)
+
+        def gain_s(i, which):
+            g = st["g" + which, i]
+            row = i + (0 if which == "u" else MODELS)
+            q0 = PE_COLS // K4
+            q = P - q0
+            nc.vector.tensor_tensor(out=g[:, :, q0:P, :], in0=st["xs", i][:].rearrange("p (q s t) -> p s q t", s=K4, t=K4),
+                                    in1=uv[:, row:row + 1, :].unsqueeze(1).to_broadcast([P, K4, q, K4]), op=MULT)
+
+        def quant(key, i, src, words):
+            bufs = 4 if key == "t" else 2
+            codes = work.tile([P, words], U32, name="c" + key, tag="c" + key, bufs=bufs, align_bytes=64)
+            scales = work.tile([P, words], U8, name="s" + key, tag="s" + key, bufs=bufs, align_bytes=64)
+            nc.vector.quantize_mx(out=codes[:].bitcast(FP8X4), scales=scales[:], in_=src)
+            st["c" + key, i] = (codes, scales)
+
+        def quant_g(i, which):
+            quant(which, i, st["g" + which, i][:].rearrange("p s q t -> p (s q t)"), D)
+
+        def gram(i, t):
+            uc, us = st["cu", i]
+            vc, vs = st["cv", i]
+            tag = "xp" if i == MODELS - 1 and t >= 2 else "gram"
+            g = psum.tile([P, D], F32, name="gram", tag=tag)
+            nc.tensor.matmul_mx(out=g[:], lhsT=vc[:, P * t:P * (t + 1)].bitcast(FP8X4), lhsT_scale=vs[:, P * t:P * (t + 1)],
+                                rhs=uc[:].bitcast(FP8X4), rhs_scale=us[:], start=True, stop=True)
+            st["gram", i, t] = g
+
+        def evac(i, t):
+            if t == 0:
+                st["pl", i] = work.tile([P, K4, D], BF16, name="pl", tag="pl")
+            pl = st["pl", i]
+            g = st["gram", i, t]
+            for a, b in ((0, t), (t + 1, K4)):
+                if a < b:
+                    nc.scalar.activation(out=pl[:, t, P * a:P * b], in_=g[:, P * a:P * b], func=COPY, scale=cs[:, i, t:t + 1])
+
+        def diag(i, t):
+            nc.vector.scalar_tensor_tensor(out=st["pl", i][:, t, P * t:P * (t + 1)], in0=st["gram", i, t][:, P * t:P * (t + 1)],
+                                           scalar=cs[:, i, t:t + 1], in1=dmask[:], op0=MULT, op1=MULT)
+
+        def inter(eng, dst, src, a, b):
+            eng(out=dst[:, a:b, :].rearrange("p (c i) t -> p c t i", i=4), in_=src[:, :, a:b].rearrange("p t (c i) -> p c t i", i=4))
+
+        def inter_p(i):
+            pi = work.tile([P, D, K4], BF16, name="pi", tag="pi", align_bytes=64)
+            st["pi", i] = pi
+            inter(nc.vector.tensor_copy, pi, st["pl", i], 0, V_PCOLS)
+            inter(nc.scalar.copy, pi, st["pl", i], V_PCOLS, D)
+
+        def quant_p(i):
+            quant("p", i, st["pi", i][:].rearrange("p d t -> p (d t)"), D)
+
+        def widen(i):
+            tw = work.tile([P, K4, F], BF16, name="tw", tag="tw")
+            for t in range(K4):
+                nc.scalar.activation(out=tw[:, t, :], in_=tb[i // 4][:, i % 4, F * t:F * (t + 1)].bitcast(FP8), func=COPY, scale=tscale[:, t:t + 1])
+            st["tw", i] = tw
+
+        def inter_t(i):
+            ti = work.tile([P, F, K4], BF16, name="ti", tag="ti", bufs=1, align_bytes=64)
+            st["ti", i] = ti
+            nc.gpsimd.tensor_scalar(out=ti[:], in0=st["tw", i][:].rearrange("p t f -> p f t"), scalar1=1.0, scalar2=0.0, op0=MULT, op1=ADD)
+
+        def quant_t(i):
+            quant("t", i, st["ti", i][:].rearrange("p f t -> p (f t)"), F)
+
+        def second(i):
+            pc, ps = st["cp", i]
+            tcd, tsc = st["ct", i]
+            for s in range(K4):
+                nc.tensor.matmul_mx(out=r[s][:], lhsT=pc[:, P * s:P * (s + 1)].bitcast(FP8X4), lhsT_scale=ps[:, P * s:P * (s + 1)],
+                                    rhs=tcd[:].bitcast(FP8X4), rhs_scale=tsc[:], start=(i == 0), stop=(i == MODELS - 1))
+
+        def has(i):
+            return 0 <= i < MODELS
+
+        last = MODELS - 1
+        with tc.manual_schedule():
+            for i in range(-1, MODELS):
+                if has(i + 1):
+                    ident_x(i + 1)
+                if has(i - 1):
+                    evac(i - 1, 0)
+                    evac(i - 1, 1)
+                if has(i - 2):
+                    quant_p(i - 2)
+                    second(i - 2)
+                if has(i):
+                    quant_t(i)
+                if has(i + 1):
+                    if i == -1:
+                        scal_x(0)
+                        widen(0)
+                        inter_t(0)
+                        widen(1)
+                    else:
+                        inter_t(i + 1)
+                if has(i):
+                    gain_p(i, "u")
+                if has(i - 1):
+                    diag(i - 1, 0)
+                    diag(i - 1, 1)
+                    gram(i - 1, 2)
+                    gram(i - 1, 3)
+                if has(i):
+                    gain_p(i, "v")
+                    gain_s(i, "u")
+                    gain_s(i, "v")
+                if has(i + 1) and i >= 0:
+                    scal_x(i + 1)
+                if has(i - 1):
+                    evac(i - 1, 2)
+                    evac(i - 1, 3)
+                    diag(i - 1, 2)
+                    diag(i - 1, 3)
+                if has(i + 2) and i >= 0:
+                    widen(i + 2)
+                if has(i):
+                    quant_g(i, "u")
+                    quant_g(i, "v")
+                    gram(i, 0)
+                    gram(i, 1)
+                if has(i - 1):
+                    inter_p(i - 1)
+
+            gram(last, 2)
+            gram(last, 3)
+            quant_p(last - 1)
+            second(last - 1)
+            for t in range(3):
+                evac(last, t)
+            for t in range(K4):
+                diag(last, t)
+            nc.vector.tensor_scalar(out=st["pl", last][:, 3, 0:3 * P], in0=st["gram", last, 3][:, 0:3 * P], scalar1=cs[:, last, 3:4], scalar2=None, op0=MULT)
+            pi = work.tile([P, D, K4], BF16, name="pi", tag="pi", align_bytes=64)
+            pcodes = work.tile([P, D], U32, name="cp", tag="cp", bufs=2, align_bytes=64)
+            pscales = work.tile([P, D], U8, name="sp", tag="sp", bufs=2, align_bytes=64)
+            st["cp", last] = (pcodes, pscales)
+
+            def quant_block(s):
+                nc.vector.quantize_mx(out=pcodes[:, P * s:P * (s + 1)].bitcast(FP8X4), scales=pscales[:, P * s:P * (s + 1)],
+                                      in_=pi[:, P * s:P * (s + 1), :].rearrange("p d t -> p (d t)"))
+
+            inter(nc.scalar.copy, pi, st["pl", last], 3 * P, 4 * P)
+            inter(nc.vector.tensor_copy, pi, st["pl", last], 0, P)
+            inter(nc.vector.tensor_copy, pi, st["pl", last], P, 2 * P)
+            quant_block(0)
+            inter(nc.vector.tensor_copy, pi, st["pl", last], 2 * P, 3 * P)
+            quant_block(1)
+            quant_block(2)
+            quant_block(3)
+            second(last)
+            ot = const.tile([P, K4, F], F32, name="ot")
+            for s in range(K4):
+                nc.vector.scalar_tensor_tensor(out=ot[:, s, :], in0=r[s][:], scalar=STEP, in1=w0t[:, s, :], op0=MULT, op1=ADD)
+                nc.sync.dma_start(out=out.rearrange("(q s) f -> q s f", s=K4)[:, s, :], in_=ot[:, s, :])

@@ -34,20 +34,23 @@ def tile_regmeangramdescentmerge_t_kernel(tc, x, u, v, c, tau_bytes, tau_scale, 
         psum = ctx.enter_context(tc.psum_pool(name="psum", bufs=2))
         racc = ctx.enter_context(tc.psum_pool(name="racc", bufs=1))
 
-        gains = const.tile([P, D], BF16, name="gains")
-        nc.vector.memset(gains[:].bitcast(mybir.dt.int32), 0)
-        nc.scalar.dma_start(out=gains[0:16, :], in_=u)
-        nc.scalar.dma_start(out=gains[16:32, :], in_=v)
-        nc.scalar.dma_start(out=gains[32:48, :], in_=c)
+        ctx.enter_context(tc.manual_schedule())
+        gains = []
+        for name, src in (("gu", u), ("gv", v), ("gc", c)):
+            rows = const.tile([P, D], BF16, name=name)
+            nc.vector.memset(rows[:].bitcast(mybir.dt.int32), 0)
+            nc.sync.dma_start(out=rows[0:MODELS, :], in_=src)
+            gains.append(rows)
         tscale = const.tile([P, K4], F32, name="tscale")
-        nc.scalar.dma_start(out=tscale[:], in_=tau_scale.rearrange("o (p t) z -> p (o t z)", t=K4))
+        nc.sync.dma_start(out=tscale[:], in_=tau_scale.rearrange("o (p t) z -> p (o t z)", t=K4))
 
         xt = []
         tb = []
 
         def load_x(i):
             tile = xin.tile([P, K4, D], BF16, name="xt", tag="xt")
-            nc.sync.dma_start(out=tile[:], in_=x[i].rearrange("(p t) d -> p t d", t=K4))
+            for a, b in ((0, PE_COLS), (PE_COLS, D)) if i == 0 else ((0, D),):
+                nc.sync.dma_start(out=tile[:, :, a:b], in_=x[i].rearrange("(p t) d -> p t d", t=K4)[:, :, a:b])
             xt.append(tile)
 
         def load_tau(j):
@@ -80,13 +83,20 @@ def tile_regmeangramdescentmerge_t_kernel(tc, x, u, v, c, tau_bytes, tau_scale, 
         warm = const.tile([P, 1], F32, name="warm")
         nc.scalar.activation(out=warm[:], in_=ident[:, 0:1], func=COPY)
 
-        gp = psum.tile([P, K4, P], BF16, name="gp", tag="xp")
-        for t in range(K4):
-            nc.tensor.transpose(gp[:, t, :], gains[:, t:D:K4], ident[:])
         uv = const.tile([P, 2 * MODELS, K4], BF16, name="uv")
-        nc.vector.tensor_copy(out=uv[:], in_=gp[:, :, 0:32].rearrange("p t r -> p r t"))
         cs = const.tile([P, MODELS, K4], F32, name="cs")
-        nc.vector.tensor_scalar(out=cs[:], in0=gp[:, :, 32:48].rearrange("p t r -> p r t"), scalar1=SHRINK / T, scalar2=None, op0=MULT)
+        def turn_gain(g):
+            gp = psum.tile([P, K4, P], BF16, name="gp", tag="gram")
+            for t in range(K4):
+                nc.tensor.transpose(gp[:, t, :], gains[g][:, t:D:K4], ident[:])
+            turned = gp[:, :, 0:MODELS].rearrange("p t r -> p r t")
+            if g < 2:
+                nc.vector.tensor_copy(out=uv[:, MODELS * g:MODELS * (g + 1), :], in_=turned)
+            else:
+                nc.vector.tensor_scalar(out=cs[:], in0=turned, scalar1=SHRINK / T, scalar2=None, op0=MULT)
+
+        turn_gain(0)
+        turn_gain(1)
 
         r = [racc.tile([P, F], F32, name="r%d" % s, tag="r%d" % s) for s in range(K4)]
 
@@ -123,7 +133,7 @@ def tile_regmeangramdescentmerge_t_kernel(tc, x, u, v, c, tau_bytes, tau_scale, 
                                     in1=uv[:, row:row + 1, :].unsqueeze(1).to_broadcast([P, K4, q, K4]), op=MULT)
 
         def quant(key, i, src, words):
-            bufs = 4 if key == "t" else 2
+            bufs = 3 if key == "t" else 2
             codes = work.tile([P, words], U32, name="c" + key, tag="c" + key, bufs=bufs, align_bytes=64)
             scales = work.tile([P, words], U8, name="s" + key, tag="s" + key, bufs=bufs, align_bytes=64)
             nc.vector.quantize_mx(out=codes[:].bitcast(FP8X4), scales=scales[:], in_=src)
@@ -141,27 +151,35 @@ def tile_regmeangramdescentmerge_t_kernel(tc, x, u, v, c, tau_bytes, tau_scale, 
                                 rhs=uc[:].bitcast(FP8X4), rhs_scale=us[:], start=True, stop=True)
             st["gram", i, t] = g
 
-        def evac(i, t):
-            if t == 0:
+        def plane_p(i):
+            if ("pl", i) not in st:
                 st["pl", i] = work.tile([P, K4, D], BF16, name="pl", tag="pl")
-            pl = st["pl", i]
+            return st["pl", i]
+
+        def evac(i, t):
+            pl = plane_p(i)
             g = st["gram", i, t]
             for a, b in ((0, t), (t + 1, K4)):
                 if a < b:
                     nc.scalar.activation(out=pl[:, t, P * a:P * b], in_=g[:, P * a:P * b], func=COPY, scale=cs[:, i, t:t + 1])
 
         def diag(i, t):
-            nc.vector.scalar_tensor_tensor(out=st["pl", i][:, t, P * t:P * (t + 1)], in0=st["gram", i, t][:, P * t:P * (t + 1)],
+            nc.vector.scalar_tensor_tensor(out=plane_p(i)[:, t, P * t:P * (t + 1)], in0=st["gram", i, t][:, P * t:P * (t + 1)],
                                            scalar=cs[:, i, t:t + 1], in1=dmask[:], op0=MULT, op1=MULT)
 
         def inter(eng, dst, src, a, b):
             eng(out=dst[:, a:b, :].rearrange("p (c i) t -> p c t i", i=4), in_=src[:, :, a:b].rearrange("p t (c i) -> p c t i", i=4))
 
+        def v_cols(i):
+            return 384 if i == MODELS - 2 else V_PCOLS
+
         def inter_p(i):
             pi = work.tile([P, D, K4], BF16, name="pi", tag="pi", align_bytes=64)
             st["pi", i] = pi
-            inter(nc.vector.tensor_copy, pi, st["pl", i], 0, V_PCOLS)
-            inter(nc.scalar.copy, pi, st["pl", i], V_PCOLS, D)
+            inter(nc.scalar.copy, pi, st["pl", i], v_cols(i), D)
+
+        def inter_pv(i):
+            inter(nc.vector.tensor_copy, st["pi", i], st["pl", i], 0, v_cols(i))
 
         def quant_p(i):
             quant("p", i, st["pi", i][:].rearrange("p d t -> p (d t)"), D)
@@ -175,7 +193,10 @@ def tile_regmeangramdescentmerge_t_kernel(tc, x, u, v, c, tau_bytes, tau_scale, 
         def inter_t(i):
             ti = work.tile([P, F, K4], BF16, name="ti", tag="ti", bufs=1, align_bytes=64)
             st["ti", i] = ti
-            nc.gpsimd.tensor_scalar(out=ti[:], in0=st["tw", i][:].rearrange("p t f -> p f t"), scalar1=1.0, scalar2=0.0, op0=MULT, op1=ADD)
+            if i == 0:
+                inter(nc.vector.tensor_copy, ti, st["tw", i], 0, F)
+            else:
+                nc.gpsimd.tensor_scalar(out=ti[:], in0=st["tw", i][:].rearrange("p t f -> p f t"), scalar1=1.0, scalar2=0.0, op0=MULT, op1=ADD)
 
         def quant_t(i):
             quant("t", i, st["ti", i][:].rearrange("p f t -> p (f t)"), F)
@@ -191,82 +212,91 @@ def tile_regmeangramdescentmerge_t_kernel(tc, x, u, v, c, tau_bytes, tau_scale, 
             return 0 <= i < MODELS
 
         last = MODELS - 1
-        with tc.manual_schedule():
-            for i in range(-1, MODELS):
-                if has(i + 1):
-                    ident_x(i + 1)
-                if has(i - 1):
-                    evac(i - 1, 0)
-                    evac(i - 1, 1)
-                if has(i - 2):
-                    quant_p(i - 2)
-                    second(i - 2)
-                if has(i):
-                    quant_t(i)
-                if has(i + 1):
-                    if i == -1:
-                        scal_x(0)
-                        widen(0)
-                        inter_t(0)
-                        widen(1)
-                    else:
-                        inter_t(i + 1)
-                if has(i):
-                    gain_p(i, "u")
-                if has(i - 1):
-                    diag(i - 1, 0)
-                    diag(i - 1, 1)
-                    gram(i - 1, 2)
-                    gram(i - 1, 3)
-                if has(i):
-                    gain_p(i, "v")
-                    gain_s(i, "u")
-                    gain_s(i, "v")
-                if has(i + 1) and i >= 0:
-                    scal_x(i + 1)
-                if has(i - 1):
-                    evac(i - 1, 2)
-                    evac(i - 1, 3)
-                    diag(i - 1, 2)
-                    diag(i - 1, 3)
-                if has(i + 2) and i >= 0:
-                    widen(i + 2)
-                if has(i):
-                    quant_g(i, "u")
-                    quant_g(i, "v")
-                    gram(i, 0)
-                    gram(i, 1)
-                if has(i - 1):
-                    inter_p(i - 1)
+        for i in range(-1, MODELS):
+            if has(i + 1):
+                ident_x(i + 1)
+                scal_x(i + 1)
+            if has(i - 2):
+                inter_p(i - 2)
+            if i == -1:
+                continue
+            if has(i - 1):
+                quant_t(i - 1)
+            if i == 0:
+                widen(0)
+            if i > 0:
+                inter_t(i)
+            if has(i - 2):
+                inter_pv(i - 2)
+            gain_p(i, "u")
+            gain_p(i, "v")
+            if has(i - 1):
+                diag(i - 1, 0)
+                diag(i - 1, 1)
+                evac(i - 1, 0)
+                evac(i - 1, 1)
+                gram(i - 1, 2)
+                gram(i - 1, 3)
+            gain_s(i, "u")
+            gain_s(i, "v")
+            if i == 0:
+                turn_gain(2)
+            if has(i + 1):
+                widen(i + 1)
+            if has(i - 2):
+                quant_p(i - 2)
+                second(i - 2)
+            if has(i - 1):
+                diag(i - 1, 2)
+                diag(i - 1, 3)
+                evac(i - 1, 2)
+                evac(i - 1, 3)
+            quant_g(i, "u")
+            if i == 0:
+                inter_t(0)
+            quant_g(i, "v")
+            gram(i, 0)
+            gram(i, 1)
 
-            gram(last, 2)
-            gram(last, 3)
-            quant_p(last - 1)
-            second(last - 1)
-            for t in range(3):
-                evac(last, t)
-            for t in range(K4):
-                diag(last, t)
-            nc.vector.tensor_scalar(out=st["pl", last][:, 3, 0:3 * P], in0=st["gram", last, 3][:, 0:3 * P], scalar1=cs[:, last, 3:4], scalar2=None, op0=MULT)
-            pi = work.tile([P, D, K4], BF16, name="pi", tag="pi", align_bytes=64)
-            pcodes = work.tile([P, D], U32, name="cp", tag="cp", bufs=2, align_bytes=64)
-            pscales = work.tile([P, D], U8, name="sp", tag="sp", bufs=2, align_bytes=64)
-            st["cp", last] = (pcodes, pscales)
+        quant_t(last)
+        inter_p(last - 1)
+        inter_pv(last - 1)
+        gram(last, 2)
+        gram(last, 3)
 
-            def quant_block(s):
-                nc.vector.quantize_mx(out=pcodes[:, P * s:P * (s + 1)].bitcast(FP8X4), scales=pscales[:, P * s:P * (s + 1)],
-                                      in_=pi[:, P * s:P * (s + 1), :].rearrange("p d t -> p (d t)"))
+        def evac_part(t, a, b):
+            nc.scalar.activation(out=plane_p(last)[:, t, P * a:P * b], in_=st["gram", last, t][:, P * a:P * b], func=COPY, scale=cs[:, last, t:t + 1])
 
-            inter(nc.scalar.copy, pi, st["pl", last], 3 * P, 4 * P)
-            inter(nc.vector.tensor_copy, pi, st["pl", last], 0, P)
-            inter(nc.vector.tensor_copy, pi, st["pl", last], P, 2 * P)
-            quant_block(0)
-            inter(nc.vector.tensor_copy, pi, st["pl", last], 2 * P, 3 * P)
-            quant_block(1)
-            quant_block(2)
-            quant_block(3)
-            second(last)
-            ot = const.tile([P, K4, F], F32, name="ot")
-            for s in range(K4):
-                nc.vector.scalar_tensor_tensor(out=ot[:, s, :], in0=r[s][:], scalar=STEP, in1=w0t[:, s, :], op0=MULT, op1=ADD)
-                nc.sync.dma_start(out=out.rearrange("(q s) f -> q s f", s=K4)[:, s, :], in_=ot[:, s, :])
+        diag(last, 1)
+        evac_part(0, 1, 2)
+        diag(last, 0)
+        evac_part(1, 0, 1)
+        diag(last, 2)
+        evac_part(2, 0, 2)
+        nc.vector.tensor_scalar(out=plane_p(last)[:, 3, 0:3 * P], in0=st["gram", last, 3][:, 0:3 * P], scalar1=cs[:, last, 3:4], scalar2=None, op0=MULT)
+        diag(last, 3)
+        evac_part(0, 2, 4)
+        evac_part(1, 2, 4)
+        evac_part(2, 3, 4)
+        quant_p(last - 1)
+        second(last - 1)
+        pi = work.tile([P, D, K4], BF16, name="pi", tag="pi", align_bytes=64)
+        pcodes = work.tile([P, D], U32, name="cp", tag="cp", bufs=2, align_bytes=64)
+        pscales = work.tile([P, D], U8, name="sp", tag="sp", bufs=2, align_bytes=64)
+        st["cp", last] = (pcodes, pscales)
+
+        def quant_blocks(a, b):
+            nc.vector.quantize_mx(out=pcodes[:, P * a:P * b].bitcast(FP8X4), scales=pscales[:, P * a:P * b],
+                                  in_=pi[:, P * a:P * b, :].rearrange("p d t -> p (d t)"))
+
+        inter(nc.scalar.copy, pi, st["pl", last], 3 * P, 4 * P)
+        inter(nc.vector.tensor_copy, pi, st["pl", last], 0, P)
+        inter(nc.vector.tensor_copy, pi, st["pl", last], P, 2 * P)
+        inter(nc.vector.tensor_copy, pi, st["pl", last], 2 * P, 3 * P)
+        quant_blocks(0, 2)
+        quant_blocks(2, 4)
+        second(last)
+        ot = const.tile([P, K4, F], F32, name="ot")
+        for s in range(K4):
+            nc.vector.scalar_tensor_tensor(out=ot[:, s, :], in0=r[s][:], scalar=STEP, in1=w0t[:, s, :], op0=MULT, op1=ADD)
+            nc.sync.dma_start(out=out.rearrange("(q s) f -> q s f", s=K4)[:, s, :], in_=ot[:, s, :])

@@ -21,8 +21,11 @@ MULT = mybir.AluOpType.mult
 ADD = mybir.AluOpType.add
 COPY = mybir.ActivationFunctionType.Copy
 
-PE_COLS = 256
-V_PCOLS = 192
+WARM = 4
+HALF = D // 2
+G_PCOLS = 224
+V_TAIL = 192
+V_PCOLS = 0
 
 
 def tile_regmeangramdescentmerge_t_kernel(tc, x, u, v, c, tau_bytes, tau_scale, w0, out):
@@ -35,6 +38,28 @@ def tile_regmeangramdescentmerge_t_kernel(tc, x, u, v, c, tau_bytes, tau_scale, 
         racc = ctx.enter_context(tc.psum_pool(name="racc", bufs=1))
 
         ctx.enter_context(tc.manual_schedule())
+        first = []
+        for name, src in (("fu", u), ("fv", v)):
+            first.append(const.tile([P, 1, K4], BF16, name=name))
+            nc.sync.dma_start(out=first[-1][:], in_=src[0:1].rearrange("o (p t) -> p o t", t=K4))
+        xt = []
+        xb = []
+        tb = []
+
+        def load_x(i):
+            tile = xin.tile([P, K4, HALF], BF16, name="xt", tag="xt")
+            nc.sync.dma_start(out=tile[:], in_=x[i].rearrange("(p t) d -> p t d", t=K4)[:, :, 0:HALF])
+            xt.append(tile)
+            tile = xin.tile([P, K4, HALF], BF16, name="xb", tag="xb")
+            nc.sync.dma_start(out=tile[:], in_=x[i].rearrange("(b p) d -> p b d", p=P)[:, :, HALF:D])
+            xb.append(tile)
+
+        def load_tau(j):
+            tile = const.tile([P, 4, K4 * F], U8, name="tb%d" % j, tag="tb%d" % j)
+            nc.sync.dma_start(out=tile[:], in_=tau_bytes[4 * j:4 * j + 4].rearrange("i (p t) f -> p i (t f)", t=K4))
+            tb.append(tile)
+
+        load_x(0)
         gains = []
         for name, src in (("gu", u), ("gv", v), ("gc", c)):
             rows = const.tile([P, D], BF16, name=name)
@@ -44,21 +69,6 @@ def tile_regmeangramdescentmerge_t_kernel(tc, x, u, v, c, tau_bytes, tau_scale, 
         tscale = const.tile([P, K4], F32, name="tscale")
         nc.sync.dma_start(out=tscale[:], in_=tau_scale.rearrange("o (p t) z -> p (o t z)", t=K4))
 
-        xt = []
-        tb = []
-
-        def load_x(i):
-            tile = xin.tile([P, K4, D], BF16, name="xt", tag="xt")
-            for a, b in ((0, PE_COLS), (PE_COLS, D)) if i == 0 else ((0, D),):
-                nc.sync.dma_start(out=tile[:, :, a:b], in_=x[i].rearrange("(p t) d -> p t d", t=K4)[:, :, a:b])
-            xt.append(tile)
-
-        def load_tau(j):
-            tile = const.tile([P, 4, K4 * F], U8, name="tb%d" % j, tag="tb%d" % j)
-            nc.sync.dma_start(out=tile[:], in_=tau_bytes[4 * j:4 * j + 4].rearrange("i (p t) f -> p i (t f)", t=K4))
-            tb.append(tile)
-
-        load_x(0)
         load_x(1)
         load_tau(0)
         for i in range(2, 6):
@@ -77,6 +87,10 @@ def tile_regmeangramdescentmerge_t_kernel(tc, x, u, v, c, tau_bytes, tau_scale, 
 
         ident = const.tile([P, P], BF16, name="ident")
         make_identity(nc, ident[:])
+        identf = const.tile([P, P], F32, name="identf")
+        make_identity(nc, identf[:])
+        perm = const.tile([P, K4, P // K4], F32, name="perm")
+        nc.vector.tensor_copy(out=perm[:], in_=identf[:].rearrange("p (q s) -> p s q", s=K4))
         dmask = const.tile([P, P], F32, name="dmask")
         nc.vector.tensor_scalar(out=dmask[:], in0=ident[:], scalar1=1.0 / SHRINK - 1.0, scalar2=1.0, op0=MULT, op1=ADD)
 
@@ -85,52 +99,76 @@ def tile_regmeangramdescentmerge_t_kernel(tc, x, u, v, c, tau_bytes, tau_scale, 
 
         uv = const.tile([P, 2 * MODELS, K4], BF16, name="uv")
         cs = const.tile([P, MODELS, K4], F32, name="cs")
-        def turn_gain(g):
-            gp = psum.tile([P, K4, P], BF16, name="gp", tag="gram")
+        def turn_gains():
+            gp = psum.tile([P, 2, K4, P], BF16, name="gp", tag="gram")
+            for w in range(2):
+                for t in range(K4):
+                    nc.tensor.transpose(gp[:, w, t, :], gains[w][:, t:D:K4], ident[:])
+            cp = psum.tile([P, K4, P], BF16, name="cp0", tag="gram")
             for t in range(K4):
-                nc.tensor.transpose(gp[:, t, :], gains[g][:, t:D:K4], ident[:])
-            turned = gp[:, :, 0:MODELS].rearrange("p t r -> p r t")
-            if g < 2:
-                nc.vector.tensor_copy(out=uv[:, MODELS * g:MODELS * (g + 1), :], in_=turned)
-            else:
-                nc.vector.tensor_scalar(out=cs[:], in0=turned, scalar1=SHRINK / T, scalar2=None, op0=MULT)
+                nc.tensor.transpose(cp[:, t, :], gains[2][:, t:D:K4], ident[:])
+            return gp, cp
 
-        turn_gain(0)
-        turn_gain(1)
+        def copy_gains(gp, cp):
+            nc.vector.tensor_copy(out=uv[:].rearrange("p (w r) t -> p w r t", w=2), in_=gp[:, :, :, 0:MODELS].rearrange("p w t r -> p w r t"))
+            nc.vector.tensor_scalar(out=cs[:], in0=cp[:, :, 0:MODELS].rearrange("p t r -> p r t"), scalar1=SHRINK / T, scalar2=None, op0=MULT)
+
+        zero = const.tile([P, D], BF16, name="zero")
+        nc.vector.memset(zero[:].bitcast(mybir.dt.int32), 0)
+        for k in range(WARM):
+            wp = psum.tile([P, D], F32, name="wp", tag="gram")
+            nc.tensor.matmul(wp[:], lhsT=zero[:, 0:P], rhs=zero[:], start=True, stop=True)
 
         r = [racc.tile([P, F], F32, name="r%d" % s, tag="r%d" % s) for s in range(K4)]
 
         st = {}
 
         def ident_x(i):
-            xp = psum.tile([P, PE_COLS * K4], BF16, name="xp", tag="xp")
-            for h in range(PE_COLS // P):
+            xp = psum.tile([P, HALF * K4], BF16, name="xp", tag="xp", bufs=1)
+            for h in range(2):
                 nc.tensor.matmul(xp[:, 512 * h:512 * (h + 1)], lhsT=ident[:],
                                  rhs=xt[i][:, :, P * h:P * (h + 1)].rearrange("p t d -> p d t"), start=True, stop=True)
             st["xp", i] = xp
 
-        def scal_x(i):
-            n = D - PE_COLS
-            xs = work.tile([P, n * K4], BF16, name="xs", tag="xs")
-            nc.scalar.copy(out=xs[:].rearrange("p (c i t) -> p c t i", i=4, t=K4),
-                           in_=xt[i][:, :, PE_COLS:D].rearrange("p t (c i) -> p c t i", i=4))
+        def turn_x(i):
+            xf = psum.tile([P, 2, T], BF16, name="xf", tag="xw", bufs=1)
+            for h in range(2):
+                for b in range(K4):
+                    nc.tensor.transpose(xf[:, h, P * b:P * (b + 1)], xb[i][:, b, P * h:P * (h + 1)], ident[:])
+            st["xf", i] = xf
+
+        def copy_x(i):
+            xs = work.tile([P, 2, 2, P], F32, name="xs", tag="xs")
+            nc.scalar.copy(out=xs[:], in_=st["xf", i][:].bitcast(F32).rearrange("d h (p w) -> d h w p", w=2))
             st["xs", i] = xs
 
-        def gain_p(i, which):
-            g = work.tile([P, K4, P, K4], BF16, name="g" + which, tag="g" + which, align_bytes=64)
-            st["g" + which, i] = g
-            row = i + (0 if which == "u" else MODELS)
-            q = PE_COLS // K4
-            nc.vector.tensor_tensor(out=g[:, :, 0:q, :], in0=st["xp", i][:].rearrange("p (q s t) -> p s q t", s=K4, t=K4),
-                                    in1=uv[:, row:row + 1, :].unsqueeze(1).to_broadcast([P, K4, q, K4]), op=MULT)
+        def back_x(i):
+            xw = psum.tile([P, 2, K4, HALF // K4], F32, name="xw", tag="xw", bufs=1)
+            for h in range(2):
+                for w in range(2):
+                    nc.tensor.transpose(xw[:, w, :, 32 * h:32 * (h + 1)], st["xs", i][:, h, w, :], perm[:].rearrange("p s q -> p (s q)"))
+            st["xw", i] = xw
 
-        def gain_s(i, which):
-            g = st["g" + which, i]
-            row = i + (0 if which == "u" else MODELS)
-            q0 = PE_COLS // K4
-            q = P - q0
-            nc.vector.tensor_tensor(out=g[:, :, q0:P, :], in0=st["xs", i][:].rearrange("p (q s t) -> p s q t", s=K4, t=K4),
-                                    in1=uv[:, row:row + 1, :].unsqueeze(1).to_broadcast([P, K4, q, K4]), op=MULT)
+        def gain_tile(i, which):
+            if ("g", i) not in st:
+                st["g", i] = work.tile([P, 2, K4, P, K4], BF16, name="g", tag="g", align_bytes=64)
+            return st["g", i][:, "uv".index(which)]
+
+        def gain_of(i, which):
+            w = "uv".index(which)
+            return first[w][:] if i == 0 else uv[:, i + MODELS * w:i + MODELS * w + 1, :]
+
+        def gain_p(i, which):
+            q = HALF // K4
+            nc.vector.tensor_tensor(out=gain_tile(i, which)[:, :, 0:q, :], in0=st["xp", i][:].rearrange("p (q s t) -> p s q t", s=K4, t=K4),
+                                    in1=gain_of(i, which).unsqueeze(1).to_broadcast([P, K4, q, K4]), op=MULT)
+
+        def gain_w(i, which):
+            q = HALF // K4
+            gain = gain_of(i, which).rearrange("p o (w e) -> p o w e", e=2).unsqueeze(1)
+            nc.vector.tensor_tensor(out=gain_tile(i, which)[:, :, q:P, :].rearrange("p s q (w e) -> p s q w e", e=2),
+                                    in0=st["xw", i][:].bitcast(BF16).rearrange("p w s (q e) -> p s q w e", e=2),
+                                    in1=gain.to_broadcast([P, K4, q, 2, 2]), op=MULT)
 
         def quant(key, i, src, words):
             bufs = 3 if key == "t" else 2
@@ -139,16 +177,15 @@ def tile_regmeangramdescentmerge_t_kernel(tc, x, u, v, c, tau_bytes, tau_scale, 
             nc.vector.quantize_mx(out=codes[:].bitcast(FP8X4), scales=scales[:], in_=src)
             st["c" + key, i] = (codes, scales)
 
-        def quant_g(i, which):
-            quant(which, i, st["g" + which, i][:].rearrange("p s q t -> p (s q t)"), D)
+        def quant_g(i):
+            quant("g", i, st["g", i][:].rearrange("p w s q t -> p (w s q t)"), 2 * D)
 
         def gram(i, t):
-            uc, us = st["cu", i]
-            vc, vs = st["cv", i]
-            tag = "xp" if i == MODELS - 1 and t >= 2 else "gram"
-            g = psum.tile([P, D], F32, name="gram", tag=tag)
-            nc.tensor.matmul_mx(out=g[:], lhsT=vc[:, P * t:P * (t + 1)].bitcast(FP8X4), lhsT_scale=vs[:, P * t:P * (t + 1)],
-                                rhs=uc[:].bitcast(FP8X4), rhs_scale=us[:], start=True, stop=True)
+            gc, gs = st["cg", i]
+            tag = ("gram", "gram", "xp", "xw")[t] if i == MODELS - 1 else "gram"
+            g = psum.tile([P, D], F32, name="gram", tag=tag, bufs=2 if tag == "gram" else 1)
+            nc.tensor.matmul_mx(out=g[:], lhsT=gc[:, D + P * t:D + P * (t + 1)].bitcast(FP8X4), lhsT_scale=gs[:, D + P * t:D + P * (t + 1)],
+                                rhs=gc[:, 0:D].bitcast(FP8X4), rhs_scale=gs[:, 0:D], start=True, stop=True)
             st["gram", i, t] = g
 
         def plane_p(i):
@@ -171,15 +208,23 @@ def tile_regmeangramdescentmerge_t_kernel(tc, x, u, v, c, tau_bytes, tau_scale, 
             eng(out=dst[:, a:b, :].rearrange("p (c i) t -> p c t i", i=4), in_=src[:, :, a:b].rearrange("p t (c i) -> p c t i", i=4))
 
         def v_cols(i):
-            return 384 if i == MODELS - 2 else V_PCOLS
+            return V_TAIL if i == MODELS - 2 else V_PCOLS
+
+        def packed_p(i):
+            if ("pi", i) not in st:
+                st["pi", i] = work.tile([P, D, K4], BF16, name="pi", tag="pi", align_bytes=64)
+            return st["pi", i]
 
         def inter_p(i):
-            pi = work.tile([P, D, K4], BF16, name="pi", tag="pi", align_bytes=64)
-            st["pi", i] = pi
-            inter(nc.scalar.copy, pi, st["pl", i], v_cols(i), D)
+            inter(nc.scalar.copy, packed_p(i), plane_p(i), G_PCOLS + v_cols(i), D)
+
+        def inter_pg(i):
+            nc.gpsimd.tensor_scalar(out=packed_p(i)[:, 0:G_PCOLS, :], in0=plane_p(i)[:, :, 0:G_PCOLS].rearrange("p t d -> p d t"),
+                                    scalar1=1.0, scalar2=0.0, op0=MULT, op1=ADD)
 
         def inter_pv(i):
-            inter(nc.vector.tensor_copy, st["pi", i], st["pl", i], 0, v_cols(i))
+            if v_cols(i):
+                inter(nc.vector.tensor_copy, packed_p(i), plane_p(i), G_PCOLS, G_PCOLS + v_cols(i))
 
         def quant_p(i):
             quant("p", i, st["pi", i][:].rearrange("p d t -> p (d t)"), D)
@@ -201,10 +246,10 @@ def tile_regmeangramdescentmerge_t_kernel(tc, x, u, v, c, tau_bytes, tau_scale, 
         def quant_t(i):
             quant("t", i, st["ti", i][:].rearrange("p f t -> p (f t)"), F)
 
-        def second(i):
+        def second(i, blocks=range(4)):
             pc, ps = st["cp", i]
             tcd, tsc = st["ct", i]
-            for s in range(K4):
+            for s in blocks:
                 nc.tensor.matmul_mx(out=r[s][:], lhsT=pc[:, P * s:P * (s + 1)].bitcast(FP8X4), lhsT_scale=ps[:, P * s:P * (s + 1)],
                                     rhs=tcd[:].bitcast(FP8X4), rhs_scale=tsc[:], start=(i == 0), stop=(i == MODELS - 1))
 
@@ -212,91 +257,120 @@ def tile_regmeangramdescentmerge_t_kernel(tc, x, u, v, c, tau_bytes, tau_scale, 
             return 0 <= i < MODELS
 
         last = MODELS - 1
-        for i in range(-1, MODELS):
-            if has(i + 1):
-                ident_x(i + 1)
-                scal_x(i + 1)
-            if has(i - 2):
-                inter_p(i - 2)
-            if i == -1:
-                continue
-            if has(i - 1):
-                quant_t(i - 1)
-            if i == 0:
-                widen(0)
-            if i > 0:
-                inter_t(i)
-            if has(i - 2):
-                inter_pv(i - 2)
-            gain_p(i, "u")
-            gain_p(i, "v")
-            if has(i - 1):
-                diag(i - 1, 0)
-                diag(i - 1, 1)
-                evac(i - 1, 0)
-                evac(i - 1, 1)
-                gram(i - 1, 2)
-                gram(i - 1, 3)
-            gain_s(i, "u")
-            gain_s(i, "v")
-            if i == 0:
-                turn_gain(2)
-            if has(i + 1):
-                widen(i + 1)
-            if has(i - 2):
-                quant_p(i - 2)
-                second(i - 2)
-            if has(i - 1):
-                diag(i - 1, 2)
-                diag(i - 1, 3)
-                evac(i - 1, 2)
-                evac(i - 1, 3)
-            quant_g(i, "u")
-            if i == 0:
-                inter_t(0)
-            quant_g(i, "v")
-            gram(i, 0)
-            gram(i, 1)
-
-        quant_t(last)
-        inter_p(last - 1)
-        inter_pv(last - 1)
-        gram(last, 2)
-        gram(last, 3)
-
         def evac_part(t, a, b):
             nc.scalar.activation(out=plane_p(last)[:, t, P * a:P * b], in_=st["gram", last, t][:, P * a:P * b], func=COPY, scale=cs[:, last, t:t + 1])
 
-        diag(last, 1)
-        evac_part(0, 1, 2)
-        diag(last, 0)
-        evac_part(1, 0, 1)
-        diag(last, 2)
-        evac_part(2, 0, 2)
-        nc.vector.tensor_scalar(out=plane_p(last)[:, 3, 0:3 * P], in0=st["gram", last, 3][:, 0:3 * P], scalar1=cs[:, last, 3:4], scalar2=None, op0=MULT)
-        diag(last, 3)
-        evac_part(0, 2, 4)
-        evac_part(1, 2, 4)
-        evac_part(2, 3, 4)
-        quant_p(last - 1)
-        second(last - 1)
-        pi = work.tile([P, D, K4], BF16, name="pi", tag="pi", align_bytes=64)
-        pcodes = work.tile([P, D], U32, name="cp", tag="cp", bufs=2, align_bytes=64)
-        pscales = work.tile([P, D], U8, name="sp", tag="sp", bufs=2, align_bytes=64)
+        pi = work.tile([P, D, K4], BF16, name="pl15", tag="pi15", bufs=1, align_bytes=64)
+        pcodes = work.tile([P, D], U32, name="pc15", tag="pc15", bufs=1, align_bytes=64)
+        pscales = work.tile([P, D], U8, name="ps15", tag="ps15", bufs=1, align_bytes=64)
         st["cp", last] = (pcodes, pscales)
+        ot = const.tile([P, K4, F], F32, name="ot")
 
         def quant_blocks(a, b):
             nc.vector.quantize_mx(out=pcodes[:, P * a:P * b].bitcast(FP8X4), scales=pscales[:, P * a:P * b],
                                   in_=pi[:, P * a:P * b, :].rearrange("p d t -> p (d t)"))
 
-        inter(nc.scalar.copy, pi, st["pl", last], 3 * P, 4 * P)
-        inter(nc.vector.tensor_copy, pi, st["pl", last], 0, P)
-        inter(nc.vector.tensor_copy, pi, st["pl", last], P, 2 * P)
-        inter(nc.vector.tensor_copy, pi, st["pl", last], 2 * P, 3 * P)
-        quant_blocks(0, 2)
-        quant_blocks(2, 4)
-        second(last)
-        ot = const.tile([P, K4, F], F32, name="ot")
-        for s in range(K4):
+        def second_blocks(a, b):
+            second(last, range(a, b))
+
+        def merge(s):
             nc.vector.scalar_tensor_tensor(out=ot[:, s, :], in0=r[s][:], scalar=STEP, in1=w0t[:, s, :], op0=MULT, op1=ADD)
             nc.sync.dma_start(out=out.rearrange("(q s) f -> q s f", s=K4)[:, s, :], in_=ot[:, s, :])
+
+        for i in range(-1, MODELS - 1):
+            if has(i - 1): quant_t(i - 1)
+            if has(i): gain_p(i, "u")
+            if has(i): gain_p(i, "v")
+            if i == -1: ident_x(0)
+            if has(i - 2): diag(i - 2, 2)
+            if has(i - 2): inter_pv(i - 2)
+            if has(i + 1) and i >= 0: widen(i + 1)
+            if has(i - 1): gram(i - 1, 0)
+            if i == -1: turn_x(0)
+            if i > 0: inter_t(i)
+            if has(i - 2): diag(i - 2, 3)
+            if has(i - 2): inter_p(i - 2)
+            if i == 0: copy_gains(*turned)
+            if has(i - 1): gram(i - 1, 1)
+            if has(i + 1) and i >= 0: ident_x(i + 1)
+            if has(i): gain_w(i, "v")
+            if has(i): gain_w(i, "u")
+            if has(i - 1): diag(i - 1, 0)
+            if has(i + 1) and i >= 0: turn_x(i + 1)
+            if has(i - 1): diag(i - 1, 1)
+            if has(i - 1): evac(i - 1, 0)
+            if i == -1: turned = turn_gains()
+            if has(i - 1): evac(i - 1, 1)
+            if has(i - 2): inter_pg(i - 2)
+            if has(i): quant_g(i)
+            if i == -1: copy_x(0)
+            if has(i + 1) and i >= 0: copy_x(i + 1)
+            if i == -1: widen(0)
+            if has(i - 1): gram(i - 1, 2)
+            if i == -1: back_x(0)
+            if i == 0: inter_t(0)
+            if has(i - 1): evac(i - 1, 2)
+            if has(i - 1): gram(i - 1, 3)
+            if has(i + 1) and i >= 0: back_x(i + 1)
+            if has(i - 2): quant_p(i - 2)
+            if has(i - 1): evac(i - 1, 3)
+            if has(i - 2): second(i - 2)
+
+        quant_t(last - 1)
+        gain_p(last, "u")
+        diag(last - 2, 2)
+        diag(last - 2, 3)
+        gain_w(last, "u")
+        gram(last - 1, 0)
+        gain_w(last, "v")
+        gain_p(last, "v")
+        inter_t(last)
+        evac(last - 1, 0)
+        gram(last - 1, 1)
+        evac(last - 1, 1)
+        diag(last - 1, 0)
+        gram(last - 1, 2)
+        inter_pg(last - 2)
+        diag(last - 1, 1)
+        quant_g(last)
+        inter_p(last - 2)
+        gram(last - 1, 3)
+        evac(last - 1, 2)
+        gram(last, 2)
+        gram(last, 3)
+        evac(last - 1, 3)
+        quant_p(last - 2)
+        diag(last - 1, 2)
+        gram(last, 0)
+        diag(last - 1, 3)
+        diag(last, 2)
+        gram(last, 1)
+        inter_p(last - 1)
+        evac_part(2, 0, 2)
+        nc.vector.tensor_scalar(out=plane_p(last)[:, 3, 0:3 * P], in0=st["gram", last, 3][:, 0:3 * P], scalar1=cs[:, last, 3:4], scalar2=None, op0=MULT)
+        inter_pg(last - 1)
+        diag(last, 0)
+        evac_part(0, 2, 4)
+        evac_part(2, 3, 4)
+        diag(last, 3)
+        diag(last, 1)
+        evac_part(1, 2, 4)
+        inter_pv(last - 1)
+        quant_t(last)
+        second(last - 2)
+        quant_p(last - 1)
+        evac_part(0, 1, 2)
+        evac_part(1, 0, 1)
+        inter(nc.vector.tensor_copy, pi, plane_p(last), 2 * P, 3 * P)
+        inter(nc.vector.tensor_copy, pi, plane_p(last), 0, P)
+        inter(nc.vector.tensor_copy, pi, plane_p(last), P, 2 * P)
+        inter(nc.scalar.copy, pi, plane_p(last), 3 * P, 4 * P)
+        second(last - 1)
+        quant_blocks(2, 4)
+        second_blocks(2, 4)
+        quant_blocks(0, 2)
+        second_blocks(0, 2)
+        merge(2)
+        merge(0)
+        merge(1)
+        merge(3)

@@ -23,7 +23,7 @@ COPY = mybir.ActivationFunctionType.Copy
 
 WARM = 4
 HALF = D // 2
-G_PCOLS = 224
+G_PCOLS = 192
 V_TAIL = 192
 V_PCOLS = 0
 
@@ -279,98 +279,98 @@ def tile_regmeangramdescentmerge_t_kernel(tc, x, u, v, c, tau_bytes, tau_scale, 
 
         for i in range(-1, MODELS - 1):
             if has(i - 1): quant_t(i - 1)
-            if has(i): gain_p(i, "u")
             if has(i): gain_p(i, "v")
+            if has(i): gain_p(i, "u")
             if i == -1: ident_x(0)
             if has(i - 2): diag(i - 2, 2)
-            if has(i - 2): inter_pv(i - 2)
-            if has(i + 1) and i >= 0: widen(i + 1)
             if has(i - 1): gram(i - 1, 0)
-            if i == -1: turn_x(0)
-            if i > 0: inter_t(i)
+            if has(i + 1) and i >= 0: widen(i + 1)
             if has(i - 2): diag(i - 2, 3)
-            if has(i - 2): inter_p(i - 2)
-            if i == 0: copy_gains(*turned)
             if has(i - 1): gram(i - 1, 1)
-            if has(i + 1) and i >= 0: ident_x(i + 1)
-            if has(i): gain_w(i, "v")
+            if i == 0: copy_gains(*turned)
+            if i == -1: turn_x(0)
+            if has(i - 2): inter_p(i - 2)
             if has(i): gain_w(i, "u")
+            if has(i + 1) and i >= 0: ident_x(i + 1)
+            if i > 0: inter_t(i)
+            if has(i): gain_w(i, "v")
             if has(i - 1): diag(i - 1, 0)
-            if has(i + 1) and i >= 0: turn_x(i + 1)
-            if has(i - 1): diag(i - 1, 1)
-            if has(i - 1): evac(i - 1, 0)
-            if i == -1: turned = turn_gains()
-            if has(i - 1): evac(i - 1, 1)
-            if has(i - 2): inter_pg(i - 2)
-            if has(i): quant_g(i)
             if i == -1: copy_x(0)
-            if has(i + 1) and i >= 0: copy_x(i + 1)
-            if i == -1: widen(0)
-            if has(i - 1): gram(i - 1, 2)
-            if i == -1: back_x(0)
             if i == 0: inter_t(0)
-            if has(i - 1): evac(i - 1, 2)
+            if i == -1: widen(0)
+            if has(i - 1): diag(i - 1, 1)
+            if has(i): quant_g(i)
+            if has(i - 1): evac(i - 1, 0)
+            if has(i + 1) and i >= 0: turn_x(i + 1)
+            if has(i - 1): evac(i - 1, 1)
+            if has(i - 1): gram(i - 1, 2)
+            if has(i - 2): inter_pg(i - 2)
+            if i == -1: turned = turn_gains()
             if has(i - 1): gram(i - 1, 3)
+            if i == -1: back_x(0)
+            if has(i + 1) and i >= 0: copy_x(i + 1)
             if has(i + 1) and i >= 0: back_x(i + 1)
+            if has(i - 2): inter_pv(i - 2)
+            if has(i - 1): evac(i - 1, 2)
             if has(i - 2): quant_p(i - 2)
             if has(i - 1): evac(i - 1, 3)
             if has(i - 2): second(i - 2)
 
         quant_t(last - 1)
-        gain_p(last, "u")
-        diag(last - 2, 2)
-        diag(last - 2, 3)
-        gain_w(last, "u")
-        gram(last - 1, 0)
-        gain_w(last, "v")
         gain_p(last, "v")
-        inter_t(last)
-        evac(last - 1, 0)
+        diag(last - 2, 2)
         gram(last - 1, 1)
+        diag(last - 2, 3)
+        gram(last - 1, 0)
         evac(last - 1, 1)
+        gain_w(last, "v")
+        evac(last - 1, 0)
+        inter_t(last)
+        gain_p(last, "u")
+        gain_w(last, "u")
+        diag(last - 1, 1)
+        gram(last - 1, 3)
         diag(last - 1, 0)
+        quant_g(last)
         gram(last - 1, 2)
         inter_pg(last - 2)
-        diag(last - 1, 1)
-        quant_g(last)
         inter_p(last - 2)
-        gram(last - 1, 3)
-        evac(last - 1, 2)
-        gram(last, 2)
-        gram(last, 3)
         evac(last - 1, 3)
         quant_p(last - 2)
-        diag(last - 1, 2)
-        gram(last, 0)
         diag(last - 1, 3)
+        evac(last - 1, 2)
+        gram(last, 2)
         diag(last, 2)
-        gram(last, 1)
+        gram(last, 3)
+        gram(last, 0)
+        diag(last - 1, 2)
         inter_p(last - 1)
-        evac_part(2, 0, 2)
-        nc.vector.tensor_scalar(out=plane_p(last)[:, 3, 0:3 * P], in0=st["gram", last, 3][:, 0:3 * P], scalar1=cs[:, last, 3:4], scalar2=None, op0=MULT)
-        inter_pg(last - 1)
-        diag(last, 0)
-        evac_part(0, 2, 4)
         evac_part(2, 3, 4)
         diag(last, 3)
-        diag(last, 1)
-        evac_part(1, 2, 4)
+        nc.vector.tensor_scalar(out=plane_p(last)[:, 3, 0:3 * P], in0=st["gram", last, 3][:, 0:3 * P], scalar1=cs[:, last, 3:4], scalar2=None, op0=MULT)
+        gram(last, 1)
+        diag(last, 0)
         inter_pv(last - 1)
-        quant_t(last)
+        evac_part(2, 0, 2)
+        inter_pg(last - 1)
+        evac_part(1, 2, 4)
         second(last - 2)
+        quant_t(last)
         quant_p(last - 1)
-        evac_part(0, 1, 2)
+        evac_part(0, 2, 4)
         evac_part(1, 0, 1)
+        diag(last, 1)
         inter(nc.vector.tensor_copy, pi, plane_p(last), 2 * P, 3 * P)
-        inter(nc.vector.tensor_copy, pi, plane_p(last), 0, P)
-        inter(nc.vector.tensor_copy, pi, plane_p(last), P, 2 * P)
+        evac_part(0, 1, 2)
         inter(nc.scalar.copy, pi, plane_p(last), 3 * P, 4 * P)
-        second(last - 1)
+        inter(nc.vector.tensor_copy, pi, plane_p(last), P, 2 * P)
         quant_blocks(2, 4)
+        second(last - 1)
+        inter(nc.vector.tensor_copy, pi, plane_p(last), 0, P)
         second_blocks(2, 4)
         quant_blocks(0, 2)
         second_blocks(0, 2)
+        merge(3)
         merge(2)
         merge(0)
         merge(1)
-        merge(3)

from contextlib import ExitStack

import concourse.mybir as mybir
from concourse.masks import make_identity

MODELS, T, D, F = 16, 512, 512, 256
FLOPS = 2 * MODELS * (T * D * D + D * D * F) + MODELS * (2 * T * D + 2 * D * D + D * F) + 2 * D * F

P = 128
K4 = 4
SHRINK = 0.8
STEP = 0.3

F32 = mybir.dt.float32
BF16 = mybir.dt.bfloat16
U32 = mybir.dt.uint32
U8 = mybir.dt.uint8
FP8 = mybir.dt.float8_e4m3fn
FP8X4 = mybir.dt.float8_e4m3fn_x4
MULT = mybir.AluOpType.mult
ADD = mybir.AluOpType.add
COPY = mybir.ActivationFunctionType.Copy

WARM = 4
HALF = D // 2
G_PCOLS = 192
V_TAIL = 192
V_PCOLS = 0


def tile_regmeangramdescentmerge_t_kernel(tc, x, u, v, c, tau_bytes, tau_scale, w0, out):
    nc = tc.nc
    with ExitStack() as ctx:
        const = ctx.enter_context(tc.tile_pool(name="const", bufs=1))
        xin = ctx.enter_context(tc.tile_pool(name="xin", bufs=MODELS))
        work = ctx.enter_context(tc.tile_pool(name="work", bufs=2))
        psum = ctx.enter_context(tc.psum_pool(name="psum", bufs=2))
        racc = ctx.enter_context(tc.psum_pool(name="racc", bufs=1))

        ctx.enter_context(tc.manual_schedule())
        first = []
        for name, src in (("fu", u), ("fv", v)):
            first.append(const.tile([P, 1, K4], BF16, name=name))
            nc.sync.dma_start(out=first[-1][:], in_=src[0:1].rearrange("o (p t) -> p o t", t=K4))
        xt = []
        xb = []
        tb = []

        def load_x(i):
            tile = xin.tile([P, K4, HALF], BF16, name="xt", tag="xt")
            nc.sync.dma_start(out=tile[:], in_=x[i].rearrange("(p t) d -> p t d", t=K4)[:, :, 0:HALF])
            xt.append(tile)
            tile = xin.tile([P, K4, HALF], BF16, name="xb", tag="xb")
            nc.sync.dma_start(out=tile[:], in_=x[i].rearrange("(b p) d -> p b d", p=P)[:, :, HALF:D])
            xb.append(tile)

        def load_tau(j):
            tile = const.tile([P, 4, K4 * F], U8, name="tb%d" % j, tag="tb%d" % j)
            nc.sync.dma_start(out=tile[:], in_=tau_bytes[4 * j:4 * j + 4].rearrange("i (p t) f -> p i (t f)", t=K4))
            tb.append(tile)

        load_x(0)
        gains = []
        for name, src in (("gu", u), ("gv", v), ("gc", c)):
            rows = const.tile([P, D], BF16, name=name)
            nc.vector.memset(rows[:].bitcast(mybir.dt.int32), 0)
            nc.sync.dma_start(out=rows[0:MODELS, :], in_=src)
            gains.append(rows)
        tscale = const.tile([P, K4], F32, name="tscale")
        nc.sync.dma_start(out=tscale[:], in_=tau_scale.rearrange("o (p t) z -> p (o t z)", t=K4))

        load_x(1)
        load_tau(0)
        for i in range(2, 6):
            load_x(i)
        load_tau(1)
        for i in range(6, 10):
            load_x(i)
        load_tau(2)
        for i in range(10, 14):
            load_x(i)
        load_tau(3)
        for i in range(14, 16):
            load_x(i)
        w0t = const.tile([P, K4, F], BF16, name="w0t")
        nc.sync.dma_start(out=w0t[:], in_=w0.rearrange("(q s) f -> q s f", s=K4))

        ident = const.tile([P, P], BF16, name="ident")
        make_identity(nc, ident[:])
        identf = const.tile([P, P], F32, name="identf")
        make_identity(nc, identf[:])
        perm = const.tile([P, K4, P // K4], F32, name="perm")
        nc.vector.tensor_copy(out=perm[:], in_=identf[:].rearrange("p (q s) -> p s q", s=K4))
        dmask = const.tile([P, P], F32, name="dmask")
        nc.vector.tensor_scalar(out=dmask[:], in0=ident[:], scalar1=1.0 / SHRINK - 1.0, scalar2=1.0, op0=MULT, op1=ADD)

        warm = const.tile([P, 1], F32, name="warm")
        nc.scalar.activation(out=warm[:], in_=ident[:, 0:1], func=COPY)

        uv = const.tile([P, 2 * MODELS, K4], BF16, name="uv")
        cs = const.tile([P, MODELS, K4], F32, name="cs")
        def turn_gains():
            gp = psum.tile([P, 2, K4, P], BF16, name="gp", tag="gram")
            for w in range(2):
                for t in range(K4):
                    nc.tensor.transpose(gp[:, w, t, :], gains[w][:, t:D:K4], ident[:])
            cp = psum.tile([P, K4, P], BF16, name="cp0", tag="gram")
            for t in range(K4):
                nc.tensor.transpose(cp[:, t, :], gains[2][:, t:D:K4], ident[:])
            return gp, cp

        def copy_gains(gp, cp):
            nc.vector.tensor_copy(out=uv[:].rearrange("p (w r) t -> p w r t", w=2), in_=gp[:, :, :, 0:MODELS].rearrange("p w t r -> p w r t"))
            nc.vector.tensor_scalar(out=cs[:], in0=cp[:, :, 0:MODELS].rearrange("p t r -> p r t"), scalar1=SHRINK / T, scalar2=None, op0=MULT)

        zero = const.tile([P, D], BF16, name="zero")
        nc.vector.memset(zero[:].bitcast(mybir.dt.int32), 0)
        for k in range(WARM):
            wp = psum.tile([P, D], F32, name="wp", tag="gram")
            nc.tensor.matmul(wp[:], lhsT=zero[:, 0:P], rhs=zero[:], start=True, stop=True)

        r = [racc.tile([P, F], F32, name="r%d" % s, tag="r%d" % s) for s in range(K4)]

        st = {}

        def ident_x(i):
            xp = psum.tile([P, HALF * K4], BF16, name="xp", tag="xp", bufs=1)
            for h in range(2):
                nc.tensor.matmul(xp[:, 512 * h:512 * (h + 1)], lhsT=ident[:],
                                 rhs=xt[i][:, :, P * h:P * (h + 1)].rearrange("p t d -> p d t"), start=True, stop=True)
            st["xp", i] = xp

        def turn_x(i):
            xf = psum.tile([P, 2, T], BF16, name="xf", tag="xw", bufs=1)
            for h in range(2):
                for b in range(K4):
                    nc.tensor.transpose(xf[:, h, P * b:P * (b + 1)], xb[i][:, b, P * h:P * (h + 1)], ident[:])
            st["xf", i] = xf

        def copy_x(i):
            xs = work.tile([P, 2, 2, P], F32, name="xs", tag="xs")
            nc.scalar.copy(out=xs[:], in_=st["xf", i][:].bitcast(F32).rearrange("d h (p w) -> d h w p", w=2))
            st["xs", i] = xs

        def back_x(i):
            xw = psum.tile([P, 2, K4, HALF // K4], F32, name="xw", tag="xw", bufs=1)
            for h in range(2):
                for w in range(2):
                    nc.tensor.transpose(xw[:, w, :, 32 * h:32 * (h + 1)], st["xs", i][:, h, w, :], perm[:].rearrange("p s q -> p (s q)"))
            st["xw", i] = xw

        def gain_tile(i, which):
            if ("g", i) not in st:
                st["g", i] = work.tile([P, 2, K4, P, K4], BF16, name="g", tag="g", align_bytes=64)
            return st["g", i][:, "uv".index(which)]

        def gain_of(i, which):
            w = "uv".index(which)
            return first[w][:] if i == 0 else uv[:, i + MODELS * w:i + MODELS * w + 1, :]

        def gain_p(i, which):
            q = HALF // K4
            nc.vector.tensor_tensor(out=gain_tile(i, which)[:, :, 0:q, :], in0=st["xp", i][:].rearrange("p (q s t) -> p s q t", s=K4, t=K4),
                                    in1=gain_of(i, which).unsqueeze(1).to_broadcast([P, K4, q, K4]), op=MULT)

        def gain_w(i, which):
            q = HALF // K4
            gain = gain_of(i, which).rearrange("p o (w e) -> p o w e", e=2).unsqueeze(1)
            nc.vector.tensor_tensor(out=gain_tile(i, which)[:, :, q:P, :].rearrange("p s q (w e) -> p s q w e", e=2),
                                    in0=st["xw", i][:].bitcast(BF16).rearrange("p w s (q e) -> p s q w e", e=2),
                                    in1=gain.to_broadcast([P, K4, q, 2, 2]), op=MULT)

        def quant(key, i, src, words):
            bufs = 3 if key == "t" else 2
            codes = work.tile([P, words], U32, name="c" + key, tag="c" + key, bufs=bufs, align_bytes=64)
            scales = work.tile([P, words], U8, name="s" + key, tag="s" + key, bufs=bufs, align_bytes=64)
            nc.vector.quantize_mx(out=codes[:].bitcast(FP8X4), scales=scales[:], in_=src)
            st["c" + key, i] = (codes, scales)

        def quant_g(i):
            quant("g", i, st["g", i][:].rearrange("p w s q t -> p (w s q t)"), 2 * D)

        def gram(i, t):
            gc, gs = st["cg", i]
            tag = ("gram", "gram", "xp", "xw")[t] if i == MODELS - 1 else "gram"
            g = psum.tile([P, D], F32, name="gram", tag=tag, bufs=2 if tag == "gram" else 1)
            nc.tensor.matmul_mx(out=g[:], lhsT=gc[:, D + P * t:D + P * (t + 1)].bitcast(FP8X4), lhsT_scale=gs[:, D + P * t:D + P * (t + 1)],
                                rhs=gc[:, 0:D].bitcast(FP8X4), rhs_scale=gs[:, 0:D], start=True, stop=True)
            st["gram", i, t] = g

        def plane_p(i):
            if ("pl", i) not in st:
                st["pl", i] = work.tile([P, K4, D], BF16, name="pl", tag="pl")
            return st["pl", i]

        def evac(i, t):
            pl = plane_p(i)
            g = st["gram", i, t]
            for a, b in ((0, t), (t + 1, K4)):
                if a < b:
                    nc.scalar.activation(out=pl[:, t, P * a:P * b], in_=g[:, P * a:P * b], func=COPY, scale=cs[:, i, t:t + 1])

        def diag(i, t):
            nc.vector.scalar_tensor_tensor(out=plane_p(i)[:, t, P * t:P * (t + 1)], in0=st["gram", i, t][:, P * t:P * (t + 1)],
                                           scalar=cs[:, i, t:t + 1], in1=dmask[:], op0=MULT, op1=MULT)

        def inter(eng, dst, src, a, b):
            eng(out=dst[:, a:b, :].rearrange("p (c i) t -> p c t i", i=4), in_=src[:, :, a:b].rearrange("p t (c i) -> p c t i", i=4))

        def v_cols(i):
            return V_TAIL if i == MODELS - 2 else V_PCOLS

        def packed_p(i):
            if ("pi", i) not in st:
                st["pi", i] = work.tile([P, D, K4], BF16, name="pi", tag="pi", align_bytes=64)
            return st["pi", i]

        def inter_p(i):
            inter(nc.scalar.copy, packed_p(i), plane_p(i), G_PCOLS + v_cols(i), D)

        def inter_pg(i):
            nc.gpsimd.tensor_scalar(out=packed_p(i)[:, 0:G_PCOLS, :], in0=plane_p(i)[:, :, 0:G_PCOLS].rearrange("p t d -> p d t"),
                                    scalar1=1.0, scalar2=0.0, op0=MULT, op1=ADD)

        def inter_pv(i):
            if v_cols(i):
                inter(nc.vector.tensor_copy, packed_p(i), plane_p(i), G_PCOLS, G_PCOLS + v_cols(i))

        def quant_p(i):
            quant("p", i, st["pi", i][:].rearrange("p d t -> p (d t)"), D)

        def widen(i):
            tw = work.tile([P, K4, F], BF16, name="tw", tag="tw")
            for t in range(K4):
                nc.scalar.activation(out=tw[:, t, :], in_=tb[i // 4][:, i % 4, F * t:F * (t + 1)].bitcast(FP8), func=COPY, scale=tscale[:, t:t + 1])
            st["tw", i] = tw

        def inter_t(i):
            ti = work.tile([P, F, K4], BF16, name="ti", tag="ti", bufs=1, align_bytes=64)
            st["ti", i] = ti
            if i == 0:
                inter(nc.vector.tensor_copy, ti, st["tw", i], 0, F)
            else:
                nc.gpsimd.tensor_scalar(out=ti[:], in0=st["tw", i][:].rearrange("p t f -> p f t"), scalar1=1.0, scalar2=0.0, op0=MULT, op1=ADD)

        def quant_t(i):
            quant("t", i, st["ti", i][:].rearrange("p f t -> p (f t)"), F)

        def second(i, blocks=range(4)):
            pc, ps = st["cp", i]
            tcd, tsc = st["ct", i]
            for s in blocks:
                nc.tensor.matmul_mx(out=r[s][:], lhsT=pc[:, P * s:P * (s + 1)].bitcast(FP8X4), lhsT_scale=ps[:, P * s:P * (s + 1)],
                                    rhs=tcd[:].bitcast(FP8X4), rhs_scale=tsc[:], start=(i == 0), stop=(i == MODELS - 1))

        def has(i):
            return 0 <= i < MODELS

        last = MODELS - 1
        def evac_part(t, a, b):
            nc.scalar.activation(out=plane_p(last)[:, t, P * a:P * b], in_=st["gram", last, t][:, P * a:P * b], func=COPY, scale=cs[:, last, t:t + 1])

        pi = work.tile([P, D, K4], BF16, name="pl15", tag="pi15", bufs=1, align_bytes=64)
        pcodes = work.tile([P, D], U32, name="pc15", tag="pc15", bufs=1, align_bytes=64)
        pscales = work.tile([P, D], U8, name="ps15", tag="ps15", bufs=1, align_bytes=64)
        st["cp", last] = (pcodes, pscales)
        ot = const.tile([P, K4, F], F32, name="ot")

        def quant_blocks(a, b):
            nc.vector.quantize_mx(out=pcodes[:, P * a:P * b].bitcast(FP8X4), scales=pscales[:, P * a:P * b],
                                  in_=pi[:, P * a:P * b, :].rearrange("p d t -> p (d t)"))

        def second_blocks(a, b):
            second(last, range(a, b))

        def merge(s):
            nc.vector.scalar_tensor_tensor(out=ot[:, s, :], in0=r[s][:], scalar=STEP, in1=w0t[:, s, :], op0=MULT, op1=ADD)
            nc.sync.dma_start(out=out.rearrange("(q s) f -> q s f", s=K4)[:, s, :], in_=ot[:, s, :])

        for i in range(-1, MODELS - 1):
            if has(i - 1): quant_t(i - 1)
            if has(i): gain_p(i, "v")
            if has(i): gain_p(i, "u")
            if i == -1: ident_x(0)
            if has(i - 2): diag(i - 2, 2)
            if has(i - 1): gram(i - 1, 0)
            if has(i + 1) and i >= 0: widen(i + 1)
            if has(i - 2): diag(i - 2, 3)
            if has(i - 1): gram(i - 1, 1)
            if i == 0: copy_gains(*turned)
            if i == -1: turn_x(0)
            if has(i - 2): inter_p(i - 2)
            if has(i): gain_w(i, "u")
            if has(i + 1) and i >= 0: ident_x(i + 1)
            if i > 0: inter_t(i)
            if has(i): gain_w(i, "v")
            if has(i - 1): diag(i - 1, 0)
            if i == -1: copy_x(0)
            if i == 0: inter_t(0)
            if i == -1: widen(0)
            if has(i - 1): diag(i - 1, 1)
            if has(i): quant_g(i)
            if has(i - 1): evac(i - 1, 0)
            if has(i + 1) and i >= 0: turn_x(i + 1)
            if has(i - 1): evac(i - 1, 1)
            if has(i - 1): gram(i - 1, 2)
            if has(i - 2): inter_pg(i - 2)
            if i == -1: turned = turn_gains()
            if has(i - 1): gram(i - 1, 3)
            if i == -1: back_x(0)
            if has(i + 1) and i >= 0: copy_x(i + 1)
            if has(i + 1) and i >= 0: back_x(i + 1)
            if has(i - 2): inter_pv(i - 2)
            if has(i - 1): evac(i - 1, 2)
            if has(i - 2): quant_p(i - 2)
            if has(i - 1): evac(i - 1, 3)
            if has(i - 2): second(i - 2)

        quant_t(last - 1)
        gain_p(last, "v")
        diag(last - 2, 2)
        gram(last - 1, 1)
        diag(last - 2, 3)
        gram(last - 1, 0)
        evac(last - 1, 1)
        gain_w(last, "v")
        evac(last - 1, 0)
        inter_t(last)
        gain_p(last, "u")
        gain_w(last, "u")
        diag(last - 1, 1)
        gram(last - 1, 3)
        diag(last - 1, 0)
        quant_g(last)
        gram(last - 1, 2)
        inter_pg(last - 2)
        inter_p(last - 2)
        evac(last - 1, 3)
        quant_p(last - 2)
        diag(last - 1, 3)
        evac(last - 1, 2)
        gram(last, 2)
        diag(last, 2)
        gram(last, 3)
        gram(last, 0)
        diag(last - 1, 2)
        inter_p(last - 1)
        evac_part(2, 3, 4)
        diag(last, 3)
        nc.vector.tensor_scalar(out=plane_p(last)[:, 3, 0:3 * P], in0=st["gram", last, 3][:, 0:3 * P], scalar1=cs[:, last, 3:4], scalar2=None, op0=MULT)
        gram(last, 1)
        diag(last, 0)
        inter_pv(last - 1)
        evac_part(2, 0, 2)
        inter_pg(last - 1)
        evac_part(1, 2, 4)
        second(last - 2)
        quant_t(last)
        quant_p(last - 1)
        evac_part(0, 2, 4)
        evac_part(1, 0, 1)
        diag(last, 1)
        inter(nc.vector.tensor_copy, pi, plane_p(last), 2 * P, 3 * P)
        evac_part(0, 1, 2)
        inter(nc.scalar.copy, pi, plane_p(last), 3 * P, 4 * P)
        inter(nc.vector.tensor_copy, pi, plane_p(last), P, 2 * P)
        quant_blocks(2, 4)
        second(last - 1)
        inter(nc.vector.tensor_copy, pi, plane_p(last), 0, P)
        second_blocks(2, 4)
        quant_blocks(0, 2)
        second_blocks(0, 2)
        merge(3)
        merge(2)
        merge(0)
        merge(1)
